import numpy as np
import ml_dtypes


def mxq(x, axis, fmt="e4m3"):
    dtype, down = {"e4m3": (ml_dtypes.float8_e4m3fn, 7), "e5m2": (ml_dtypes.float8_e5m2, 14)}[fmt]
    v = np.moveaxis(np.asarray(x, np.float32).astype(ml_dtypes.bfloat16).astype(np.float64), axis, -1)
    blocks = v.reshape(v.shape[:-1] + (-1, 32))
    amax = np.abs(blocks).max(-1, keepdims=True)
    byte = np.maximum(np.where(amax > 0, np.frexp(amax)[1] - 1 + 127, 0) - down, 1)
    scale = np.exp2(byte - 127.0)
    codes = (blocks / scale).astype(np.float32).astype(dtype).astype(np.float64)
    return np.moveaxis((codes * scale).reshape(v.shape), -1, axis)


WIDE = False


def mx_kscale(k):
    if not WIDE:
        return np.ones(k)
    levels = np.array([10, -10, 5, -5, 0])
    if k % 512:
        return np.exp2(np.random.permutation(np.resize(levels, k // 32))).repeat(32)
    a = np.empty((k // 512, 16))
    for p in range(k // 512):
        a[p, :8] = np.random.permutation(np.resize(levels, 8))
        for g in range(8):
            far = levels[np.abs(levels - a[p, g]) >= 10]
            a[p, g + 8] = far[np.random.randint(len(far))]
    return np.exp2(a.ravel()).repeat(32)


BF16 = ml_dtypes.bfloat16


def bf(x):
    return np.asarray(x, np.float32).astype(BF16)


def f64(x):
    return np.asarray(x).astype(np.float64)

def planes(Y):
    n, m = Y.shape
    b = f64(bf(Y)).reshape(n // 32, 32, m)
    amax = np.abs(b).max(1)
    byte = np.clip(np.where(amax > 0, np.frexp(amax)[1] - 1 + 127 - 7, 1), 1, 254)
    codes = (b * np.exp2(127.0 - byte)[:, None, :]).reshape(n, m).astype(np.float32).astype(ml_dtypes.float8_e4m3fn).view(np.uint8)
    words = codes.reshape(n // 512, 128, 4, m).transpose(0, 1, 3, 2)
    return np.ascontiguousarray(words), np.ascontiguousarray(byte.astype(np.uint8).reshape(n // 512, 16, m))


B, K, M, T = 1024, 512, 1024, 1024


def setup_inputs():
    s = mx_kscale(K)
    t = mx_kscale(M)
    return {
        "xf": bf(np.random.standard_normal((B, K)) * s),
        "xr": bf(np.random.standard_normal((B, K)) * s),
        "w": bf(np.random.standard_normal((K, M)) / np.sqrt(K) / s[:, None]),
        "mu": bf(np.random.standard_normal(M) * 0.5),
        "a": bf(np.random.standard_normal(M) * t),
        "r": bf(np.random.standard_normal((M, T)) * 4.0 / np.sqrt(M) / t[:, None]),
        "b": bf(np.random.standard_normal(T) * 0.3),
    }


def two_strand_log_weight(ef, er, mu):
    pooled = np.maximum(ef, er) + np.log(1.0 + np.exp(-np.abs(ef - er)))
    return pooled + mu[None, :]


def sigmoid(v):
    return 1.0 / (1.0 + np.exp(-v))


def core(xf, xr, w, mu, a, r, b):
    wq = mxq(f64(w), 0, "e4m3")
    ef = mxq(f64(xf), 1, "e4m3") @ wq
    er = mxq(f64(xr), 1, "e4m3") @ wq
    lz = two_strand_log_weight(ef, er, f64(mu))
    occ = sigmoid(lz)
    s = (occ - 0.5) * f64(a)[None, :]
    return (mxq(s, 1, "e4m3") @ mxq(f64(r), 0, "e4m3")) + f64(b)[None, :]


def reference(xf, xr, w, mu, a, r, b):
    R_out = core(xf, xr, w, mu, a, r, b)
    words, scales = planes(R_out)
    return R_out, words, scales

@@ -1,0 +1,327 @@
+from contextlib import ExitStack
+
+import math
+
+import concourse.mybir as mybir
+from concourse.masks import make_identity
+
+B, K, M, T = 1024, 512, 1024, 1024
+FLOPS = 2 * (2 * B * K * M) + 2 * B * M * T
+
+F32 = mybir.dt.float32
+BF16 = mybir.dt.bfloat16
+U32 = mybir.dt.uint32
+I32 = mybir.dt.int32
+U8 = mybir.dt.uint8
+FP8X4 = mybir.dt.float8_e4m3fn_x4
+ADD = mybir.AluOpType.add
+MULT = mybir.AluOpType.mult
+ACT = mybir.ActivationFunctionType
+
+P = 128
+KAPPA = 0.8125
+ROOT = 1.0 / math.sqrt(2.0 * KAPPA)
+
+
+def tile_twostrandmotifboltzmannoccupancyreadout_x1_kernel(tc, xf, xr, w, mu, a, r, b, out_0, out_1, out_2):
+    nc = tc.nc
+    with ExitStack() as ctx:
+        keep = ctx.enter_context(tc.tile_pool(name="keep", bufs=1))
+        ring = ctx.enter_context(tc.tile_pool(name="ring", bufs=7))
+        epool = ctx.enter_context(tc.tile_pool(name="epool", bufs=3))
+        upool = ctx.enter_context(tc.tile_pool(name="upool", bufs=2))
+        psum = ctx.enter_context(tc.psum_pool(name="psum", bufs=8))
+        ctx.enter_context(tc.manual_schedule())
+
+        def kt(shape, dtype, name):
+            return keep.tile(shape, dtype, name=name, align_bytes=64)
+
+        def grouped():
+            return ring.tile([P, 512, 4], BF16, name="grouped", align_bytes=64)
+
+        ident = kt([P, P], F32, "ident")
+        make_identity(nc, ident[:])
+        mu_raw = kt([P, 8], BF16, "mu_raw")
+        a_raw = kt([P, 8], BF16, "a_raw")
+        mu_f = kt([P, 8], F32, "mu_f")
+        a_pos = kt([P, 8], F32, "a_pos")
+        a_neg = kt([P, 8], F32, "a_neg")
+        b_all = kt([P, T], BF16, "b_all")
+
+        w_raw = [kt([P, 4, 512], BF16, "w_raw%d" % g) for g in range(2)]
+        w_codes = [kt([P, 512], U32, "w_codes%d" % g) for g in range(2)]
+        w_scales = [kt([P, 512], U8, "w_scales%d" % g) for g in range(2)]
+        x_raw = {(s, h): kt([P, 4, 512], BF16, "x_raw%d%d" % (s, h)) for s in range(2) for h in range(2)}
+        x_codes = {(s, h): kt([P, 512], U32, "x_codes%d%d" % (s, h)) for s in range(2) for h in range(2)}
+        x_scales = {(s, h): kt([P, 512], U8, "x_scales%d%d" % (s, h)) for s in range(2) for h in range(2)}
+        r_raw = [kt([P, 4, T], BF16, "r_raw%d" % g) for g in range(2)]
+        r_codes = [kt([P, T], U32, "r_codes%d" % g) for g in range(2)]
+        r_scales = [kt([P, T], U8, "r_scales%d" % g) for g in range(2)]
+        weight = [kt([P, 4, 512], F32, "weight%d" % k) for k in range(4)]
+        s_codes = [kt([P, 512], U32, "s_codes%d" % k) for k in range(4)]
+        s_scales = [kt([P, 512], U8, "s_scales%d" % k) for k in range(4)]
+        o_f32 = [kt([P, 4, T], F32, "o_f32%d" % h) for h in range(2)]
+        o_codes = [kt([P, T], U32, "o_codes%d" % h) for h in range(2)]
+        o_scales = [kt([P, T], U8, "o_scales%d" % h) for h in range(2)]
+
+        nc.scalar.dma_start(out=mu_raw[:].rearrange("p (g t) -> p g t", t=4), in_=mu.rearrange("(g p t) -> p g t", p=P, t=4))
+        nc.scalar.dma_start(out=a_raw[:].rearrange("p (g t) -> p g t", t=4), in_=a.rearrange("(g p t) -> p g t", p=P, t=4))
+
+        def load_w(g):
+            nc.sync.dma_start(out=w_raw[g][:], in_=w[:, 512 * g : 512 * g + 512].rearrange("(p j) c -> p j c", j=4))
+
+        def load_x(s, h):
+            src = (xf, xr)[s]
+            nc.sync.dma_start(out=x_raw[s, h][:], in_=src[512 * h : 512 * h + 512, :].rearrange("(p t) k -> p t k", t=4))
+
+        def load_r(g):
+            nc.sync.dma_start(out=r_raw[g][:], in_=r[512 * g : 512 * g + 512, :].rearrange("(p j) c -> p j c", j=4))
+
+        load_w(0)
+        load_x(0, 0)
+        load_w(1)
+        load_x(1, 0)
+        load_r(0)
+        load_x(0, 1)
+        load_x(1, 1)
+        load_r(1)
+        nc.sync.dma_start(out=b_all[:], in_=b.partition_broadcast(P))
+
+        nc.scalar.copy(out=mu_f[:], in_=mu_raw[:])
+        nc.scalar.mul(out=a_pos[:], in_=a_raw[:], mul=KAPPA * ROOT)
+        nc.scalar.mul(out=a_neg[:], in_=a_raw[:], mul=-KAPPA)
+
+        def quantize(codes, scales, rows):
+            nc.vector.quantize_mx(out=codes.bitcast(FP8X4), scales=scales, in_=rows.rearrange("p c j -> p (c j)"))
+
+        box = {}
+
+        def w_copy(g):
+            box["w", g] = grouped()
+            nc.vector.tensor_copy(
+                out=box["w", g][:].rearrange("p (t m) j -> p t m j", t=4),
+                in_=w_raw[g][:].rearrange("p j (m t) -> p t m j", t=4),
+            )
+
+        def w_quant(g):
+            quantize(w_codes[g][:], w_scales[g][:], box["w", g][:])
+
+        def r_copy(g, n):
+            box["r", g, n] = grouped()
+            nc.vector.tensor_copy(
+                out=box["r", g, n][:].rearrange("p (c i) j -> p c j i", i=4),
+                in_=r_raw[g][:, :, 512 * n : 512 * n + 512].rearrange("p j (c i) -> p c j i", i=4),
+            )
+
+        def r_quant(g, n):
+            cols = slice(512 * n, 512 * n + 512)
+            quantize(r_codes[g][:, cols], r_scales[g][:, cols], box["r", g, n][:])
+
+        def x_turn(s, h, copy, halves=range(2)):
+            words = x_raw[s, h][:].bitcast(F32)
+            if 0 in halves:
+                box["x", s, h] = grouped()
+            for half in halves:
+                bank = psum.tile([P, 2, 2, P], F32, name="bank")
+                for q in range(2):
+                    for u in range(2):
+                        nc.tensor.transpose(bank[:, q, u, :], words[:, 2 * half + q, u::2], ident[:])
+                copy(
+                    out=box["x", s, h][:, 256 * half : 256 * half + 256, :].bitcast(F32).rearrange("p (q n) u -> p q n u", q=2),
+                    in_=bank[:].rearrange("p q u n -> p q n u"),
+                )
+
+        def x_quant(s, h):
+            quantize(x_codes[s, h][:], x_scales[s, h][:], box["x", s, h][:])
+
+        def scores(i, strands=range(2)):
+            h, m = divmod(i, 8)
+            g, t = divmod(m, 4)
+            cols = slice(P * t, P * t + P)
+            for s in strands:
+                bank = psum.tile([P, 512], F32, name="bank")
+                nc.tensor.matmul_mx(
+                    out=bank[:],
+                    lhsT=w_codes[g][:, cols].bitcast(FP8X4),
+                    lhsT_scale=w_scales[g][:, cols],
+                    rhs=x_codes[s, h][:].bitcast(FP8X4),
+                    rhs_scale=x_scales[s, h][:],
+                    start=True,
+                    stop=True,
+                )
+                if i % 2 == 0:
+                    box["e", s] = epool.tile([P, 2, 512], F32, name="e%d" % s)
+                nc.scalar.activation(out=box["e", s][:, i % 2, :], in_=bank[:], func=ACT.Exp, bias=mu_f[:, m : m + 1])
+            if i % 2 == 1 and 1 in strands:
+                box["e", "pair", i] = (box["e", 0], box["e", 1])
+
+        def add_parts(i):
+            h, m = divmod(i, 8)
+            g, t = divmod(m, 4)
+            e0, e1 = box["e", "pair", i]
+            nc.vector.scalar_tensor_tensor(out=weight[2 * h + g][:, t - 1 : t + 1, :], in0=e0[:], scalar=1.0, in1=e1[:], op0=ADD, op1=ADD)
+
+        def root(k, lo=0, hi=512):
+            for half in range(2):
+                part = weight[k][:, 2 * half : 2 * half + 2, lo:hi]
+                nc.scalar.activation(out=part, in_=part, func=ACT.Abs_reciprocal_sqrt, scale=KAPPA)
+
+        def factor(k, on_act, lo=0, hi=512):
+            g = k % 2
+            if lo == 0:
+                box["u", k] = upool.tile([P, 4, 512], F32, name="u")
+            for t in range(4):
+                m = 4 * g + t
+                src = weight[k][:, t, lo:hi]
+                dst = box["u", k][:, t, lo:hi]
+                if t in on_act:
+                    nc.scalar.activation(out=dst, in_=src, func=ACT.Identity, scale=a_neg[:, m : m + 1], bias=a_pos[:, m : m + 1])
+                else:
+                    nc.vector.tensor_scalar(out=dst, in0=src, scalar1=a_neg[:, m : m + 1], scalar2=a_pos[:, m : m + 1], op0=MULT, op1=ADD)
+
+        def product(k, lo=0, hi=512):
+            if lo == 0:
+                box["s", k] = grouped()
+            nc.vector.scalar_tensor_tensor(
+                out=box["s", k][:, lo:hi, :],
+                in0=weight[k][:, :, lo:hi].rearrange("p t c -> p c t"),
+                scalar=ROOT,
+                in1=box["u", k][:, :, lo:hi].rearrange("p t c -> p c t"),
+                op0=ADD,
+                op1=MULT,
+            )
+
+        def s_quant(k, lo=0, hi=512):
+            quantize(s_codes[k][:, lo:hi], s_scales[k][:, lo:hi], box["s", k][:, lo:hi, :])
+
+        def readout(h, g, slices, blocks):
+            for n in blocks:
+                for t in slices:
+                    if g == 0:
+                        box["o", h, n, t] = psum.tile([P, 512], F32, name="bank")
+                    cols = slice(512 * n, 512 * n + 512)
+                    rows = slice(P * t, P * t + P)
+                    nc.tensor.matmul_mx(
+                        out=box["o", h, n, t][:],
+                        lhsT=s_codes[2 * h + g][:, rows].bitcast(FP8X4),
+                        lhsT_scale=s_scales[2 * h + g][:, rows],
+                        rhs=r_codes[g][:, cols].bitcast(FP8X4),
+                        rhs_scale=r_scales[g][:, cols],
+                        start=(g == 0),
+                        stop=(g == 1),
+                    )
+
+        def bias(h, lo, hi, slices):
+            n = lo // 512
+            for t in slices:
+                nc.vector.tensor_tensor(out=o_f32[h][:, t, lo:hi], in0=box["o", h, n, t][:, lo - 512 * n : hi - 512 * n], in1=b_all[:, lo:hi], op=ADD)
+
+        def store(h, lo, hi, slices=slice(0, 4)):
+            nc.sync.dma_start(
+                out=out_0[512 * h : 512 * h + 512, lo:hi].rearrange("(p t) c -> p t c", t=4)[:, slices, :],
+                in_=o_f32[h][:, slices, lo:hi],
+            )
+
+        def o_cast(h, lo, hi, on_act):
+            n = lo // 512
+            if lo == 512 * n:
+                box["og", h, n] = grouped()
+            dst = box["og", h, n][:, lo - 512 * n : hi - 512 * n, :].rearrange("p (c i) t -> p c t i", i=4)
+            src = o_f32[h][:, :, lo:hi].rearrange("p t (c i) -> p c t i", i=4)
+            if on_act:
+                nc.scalar.copy(out=dst, in_=src)
+            else:
+                nc.vector.tensor_copy(out=dst, in_=src)
+
+        def o_quant(h, lo, hi):
+            n = lo // 512
+            cols = slice(lo, hi)
+            quantize(o_codes[h][:, cols], o_scales[h][:, cols], box["og", h, n][:, lo - 512 * n : hi - 512 * n, :])
+            nc.sync.dma_start(
+                out=out_1[h, :, cols, :].rearrange("p c t -> p (c t)").bitcast(I32),
+                in_=o_codes[h][:, cols].bitcast(I32),
+            )
+
+        def store_scales(h, lo, hi):
+            for q in range(4):
+                nc.sync.dma_start(
+                    out=out_2[h, 4 * q : 4 * q + 4, lo:hi].bitcast(I32),
+                    in_=o_scales[h][32 * q : 32 * q + 4, lo:hi].bitcast(I32),
+                )
+
+        on_act = nc.scalar.copy
+        on_vec = nc.vector.tensor_copy
+        w_copy(0)
+        x_turn(0, 0, on_act)
+        w_quant(0)
+        w_copy(1)
+        x_turn(1, 0, on_act)
+        x_quant(0, 0)
+        w_quant(1)
+        scores(0, [0])
+        scores(1, [0])
+        x_quant(1, 0)
+        scores(0, [1])
+        scores(1, [1])
+        extra = {
+            2: [lambda: r_copy(0, 0)],
+            3: [lambda: x_turn(0, 1, on_vec)],
+            4: [lambda: r_quant(0, 0), lambda: x_turn(1, 1, on_vec), lambda: x_quant(0, 1)],
+            5: [lambda: x_quant(1, 1)],
+            6: [lambda: r_copy(0, 1)],
+            8: [lambda: r_quant(0, 1)],
+            10: [lambda: r_copy(1, 0)],
+            12: [lambda: r_quant(1, 0)],
+        }
+        for i in range(2, 16):
+            scores(i)
+            for job in extra.get(i, []):
+                job()
+            if i % 2 == 0:
+                add_parts(i - 1)
+        r_copy(1, 1)
+        add_parts(15)
+        root(0)
+        root(1)
+        factor(0, [])
+        r_quant(1, 1)
+        product(0)
+        factor(1, [2, 3])
+        root(2)
+        s_quant(0)
+        product(1)
+        readout(0, 0, range(4), range(2))
+        factor(2, [0, 1, 2, 3])
+        s_quant(1)
+        readout(0, 1, range(4), range(2))
+        root(3)
+        factor(3, [0, 1, 2, 3])
+        bias(0, 0, 512, range(4))
+        store(0, 0, 512)
+        product(2)
+        bias(0, 512, 1024, range(4))
+        store(0, 512, 1024)
+        s_quant(2)
+        readout(1, 0, range(4), range(2))
+        o_cast(0, 0, 512, True)
+        o_cast(0, 512, 1024, True)
+        product(3, 0, 256)
+        product(3, 256, 512)
+        s_quant(3, 0, 256)
+        s_quant(3, 256, 512)
+        readout(1, 1, range(4), range(2))
+        o_quant(0, 0, 512)
+        o_quant(0, 512, 1024)
+        store_scales(0, 0, 1024)
+        bias(1, 0, 512, range(4))
+        store(1, 0, 512)
+        o_cast(1, 0, 512, True)
+        for t in range(4):
+            bias(1, 512, 1024, [t])
+            store(1, 512, 1024, slice(t, t + 1))
+        o_quant(1, 0, 512)
+        o_cast(1, 512, 768, False)
+        o_cast(1, 768, 1024, True)
+        o_quant(1, 512, 768)
+        o_quant(1, 768, 1024)
+        store_scales(1, 0, 1024)

@@ -1,7 +1,5 @@
 from contextlib import ExitStack
 
-import math
-
 import concourse.mybir as mybir
 from concourse.masks import make_identity
 
@@ -15,12 +13,12 @@ I32 = mybir.dt.int32
 U8 = mybir.dt.uint8
 FP8X4 = mybir.dt.float8_e4m3fn_x4
 ADD = mybir.AluOpType.add
+SUB = mybir.AluOpType.subtract
 MULT = mybir.AluOpType.mult
 ACT = mybir.ActivationFunctionType
 
 P = 128
 KAPPA = 0.8125
-ROOT = 1.0 / math.sqrt(2.0 * KAPPA)
 
 
 def tile_twostrandmotifboltzmannoccupancyreadout_x1_kernel(tc, xf, xr, w, mu, a, r, b, out_0, out_1, out_2):
@@ -28,8 +26,7 @@ def tile_twostrandmotifboltzmannoccupancyreadout_x1_kernel(tc, xf, xr, w, mu, a,
     with ExitStack() as ctx:
         keep = ctx.enter_context(tc.tile_pool(name="keep", bufs=1))
         ring = ctx.enter_context(tc.tile_pool(name="ring", bufs=7))
-        epool = ctx.enter_context(tc.tile_pool(name="epool", bufs=3))
-        upool = ctx.enter_context(tc.tile_pool(name="upool", bufs=2))
+        epool = ctx.enter_context(tc.tile_pool(name="epool", bufs=2))
         psum = ctx.enter_context(tc.psum_pool(name="psum", bufs=8))
         ctx.enter_context(tc.manual_schedule())
 
@@ -44,7 +41,6 @@ def tile_twostrandmotifboltzmannoccupancyreadout_x1_kernel(tc, xf, xr, w, mu, a,
         mu_raw = kt([P, 8], BF16, "mu_raw")
         a_raw = kt([P, 8], BF16, "a_raw")
         mu_f = kt([P, 8], F32, "mu_f")
-        a_pos = kt([P, 8], F32, "a_pos")
         a_neg = kt([P, 8], F32, "a_neg")
         b_all = kt([P, T], BF16, "b_all")
 
@@ -57,7 +53,9 @@ def tile_twostrandmotifboltzmannoccupancyreadout_x1_kernel(tc, xf, xr, w, mu, a,
         r_raw = [kt([P, 4, T], BF16, "r_raw%d" % g) for g in range(2)]
         r_codes = [kt([P, T], U32, "r_codes%d" % g) for g in range(2)]
         r_scales = [kt([P, T], U8, "r_scales%d" % g) for g in range(2)]
-        weight = [kt([P, 4, 512], F32, "weight%d" % k) for k in range(4)]
+        weight = [kt([P, 512, 4], F32, "weight%d" % k) for k in range(4)]
+        kappa = kt([P, 1], F32, "kappa")
+        nc.gpsimd.memset(kappa[:], KAPPA)
         s_codes = [kt([P, 512], U32, "s_codes%d" % k) for k in range(4)]
         s_scales = [kt([P, 512], U8, "s_scales%d" % k) for k in range(4)]
         o_f32 = [kt([P, 4, T], F32, "o_f32%d" % h) for h in range(2)]
@@ -88,7 +86,6 @@ def tile_twostrandmotifboltzmannoccupancyreadout_x1_kernel(tc, xf, xr, w, mu, a,
         nc.sync.dma_start(out=b_all[:], in_=b.partition_broadcast(P))
 
         nc.scalar.copy(out=mu_f[:], in_=mu_raw[:])
-        nc.scalar.mul(out=a_pos[:], in_=a_raw[:], mul=KAPPA * ROOT)
         nc.scalar.mul(out=a_neg[:], in_=a_raw[:], mul=-KAPPA)
 
         def quantize(codes, scales, rows):
@@ -149,45 +146,41 @@ def tile_twostrandmotifboltzmannoccupancyreadout_x1_kernel(tc, xf, xr, w, mu, a,
                     start=True,
                     stop=True,
                 )
-                if i % 2 == 0:
-                    box["e", s] = epool.tile([P, 2, 512], F32, name="e%d" % s)
-                nc.scalar.activation(out=box["e", s][:, i % 2, :], in_=bank[:], func=ACT.Exp, bias=mu_f[:, m : m + 1])
-            if i % 2 == 1 and 1 in strands:
-                box["e", "pair", i] = (box["e", 0], box["e", 1])
+                if t == 0:
+                    box["e", i // 4, s] = epool.tile([P, 4, 512], F32, name="e%d" % s)
+                nc.scalar.activation(out=box["e", i // 4, s][:, t, :], in_=bank[:], func=ACT.Exp, bias=mu_f[:, m : m + 1])
 
-        def add_parts(i):
-            h, m = divmod(i, 8)
-            g, t = divmod(m, 4)
-            e0, e1 = box["e", "pair", i]
-            nc.vector.scalar_tensor_tensor(out=weight[2 * h + g][:, t - 1 : t + 1, :], in0=e0[:], scalar=1.0, in1=e1[:], op0=ADD, op1=ADD)
+        def add_parts(k, lo, hi):
+            parts = [box["e", k, s][:, :, lo:hi].rearrange("p t (c i) -> p c t i", i=4) for s in range(2)]
+            nc.vector.tensor_tensor(
+                out=weight[k][:, lo:hi, :].rearrange("p (c i) t -> p c t i", i=4),
+                in0=parts[0],
+                in1=parts[1],
+                op=ADD,
+            )
 
-        def root(k, lo=0, hi=512):
-            for half in range(2):
-                part = weight[k][:, 2 * half : 2 * half + 2, lo:hi]
-                nc.scalar.activation(out=part, in_=part, func=ACT.Abs_reciprocal_sqrt, scale=KAPPA)
+        def root(k, lo, hi):
+            part = weight[k][:, lo:hi, :].rearrange("p c t -> p (c t)")
+            nc.scalar.activation(out=part, in_=part, func=ACT.Abs_reciprocal_sqrt, scale=KAPPA, bias=kappa[:])
 
-        def factor(k, on_act, lo=0, hi=512):
-            g = k % 2
-            if lo == 0:
-                box["u", k] = upool.tile([P, 4, 512], F32, name="u")
-            for t in range(4):
-                m = 4 * g + t
-                src = weight[k][:, t, lo:hi]
-                dst = box["u", k][:, t, lo:hi]
-                if t in on_act:
-                    nc.scalar.activation(out=dst, in_=src, func=ACT.Identity, scale=a_neg[:, m : m + 1], bias=a_pos[:, m : m + 1])
-                else:
-                    nc.vector.tensor_scalar(out=dst, in0=src, scalar1=a_neg[:, m : m + 1], scalar2=a_pos[:, m : m + 1], op0=MULT, op1=ADD)
+        def unbound(k, lo, hi):
+            part = weight[k][:, lo:hi, :].rearrange("p c t -> p (c t)")
+            nc.scalar.activation(out=part, in_=part, func=ACT.Square)
 
-        def product(k, lo=0, hi=512):
+        def unbound_v(k, lo, hi):
+            part = weight[k][:, lo:hi, :].rearrange("p c t -> p (c t)")
+            nc.vector.tensor_tensor(out=part, in0=part, in1=part, op=MULT)
+
+        def product(k, lo, hi):
             if lo == 0:
                 box["s", k] = grouped()
+            g = k % 2
             nc.vector.scalar_tensor_tensor(
                 out=box["s", k][:, lo:hi, :],
-                in0=weight[k][:, :, lo:hi].rearrange("p t c -> p c t"),
-                scalar=ROOT,
-                in1=box["u", k][:, :, lo:hi].rearrange("p t c -> p c t"),
-                op0=ADD,
+                in0=weight[k][:, lo:hi, :],
+                scalar=0.5 / KAPPA,
+                in1=a_neg[:, 4 * g : 4 * g + 4].unsqueeze(1).to_broadcast([P, hi - lo, 4]),
+                op0=SUB,
                 op1=MULT,
             )
 
@@ -265,60 +258,77 @@ def tile_twostrandmotifboltzmannoccupancyreadout_x1_kernel(tc, xf, xr, w, mu, a,
         scores(1, [1])
         extra = {
             2: [lambda: r_copy(0, 0)],
-            3: [lambda: x_turn(0, 1, on_vec)],
-            4: [lambda: r_quant(0, 0), lambda: x_turn(1, 1, on_vec), lambda: x_quant(0, 1)],
-            5: [lambda: x_quant(1, 1)],
-            6: [lambda: r_copy(0, 1)],
-            8: [lambda: r_quant(0, 1)],
-            10: [lambda: r_copy(1, 0)],
-            12: [lambda: r_quant(1, 0)],
+            3: [lambda: r_copy(0, 1), lambda: x_turn(0, 1, on_vec), lambda: x_turn(1, 1, on_vec)],
+            4: [lambda: add_parts(0, 0, 256), lambda: x_quant(0, 1)],
+            5: [lambda: add_parts(0, 256, 512), lambda: x_quant(1, 1)],
+            6: [lambda: r_quant(0, 0)],
+            7: [lambda: r_quant(0, 1)],
+            8: [lambda: r_copy(1, 0), lambda: add_parts(1, 0, 256)],
+            9: [lambda: add_parts(1, 256, 512), lambda: r_quant(1, 0)],
+            10: [lambda: r_copy(1, 1)],
+            12: [lambda: add_parts(2, 0, 256)],
+            13: [lambda: add_parts(2, 256, 512)],
         }
         for i in range(2, 16):
             scores(i)
             for job in extra.get(i, []):
                 job()
-            if i % 2 == 0:
-                add_parts(i - 1)
-        r_copy(1, 1)
-        add_parts(15)
-        root(0)
-        root(1)
-        factor(0, [])
+        fst, snd = (0, 256), (256, 512)
+        add_parts(3, *fst)
+        add_parts(3, *snd)
         r_quant(1, 1)
-        product(0)
-        factor(1, [2, 3])
-        root(2)
+        root(0, *fst)
+        root(0, *snd)
+        unbound_v(0, *fst)
+        unbound(0, *snd)
+        product(0, *fst)
+        root(1, *fst)
+        root(1, *snd)
+        unbound(1, *fst)
+        product(0, *snd)
+        root(2, *fst)
+        unbound(1, *snd)
         s_quant(0)
-        product(1)
         readout(0, 0, range(4), range(2))
-        factor(2, [0, 1, 2, 3])
+        product(1, *fst)
+        root(2, *snd)
+        unbound(2, *fst)
+        product(1, *snd)
+        root(3, *fst)
         s_quant(1)
         readout(0, 1, range(4), range(2))
-        root(3)
-        factor(3, [0, 1, 2, 3])
-        bias(0, 0, 512, range(4))
+        unbound(2, *snd)
+        product(2, *fst)
+        bias(0, 0, 512, range(3))
+        root(3, *snd)
+        unbound(3, *fst)
+        product(2, *snd)
+        bias(0, 0, 512, range(3, 4))
         store(0, 0, 512)
-        product(2)
-        bias(0, 512, 1024, range(4))
-        store(0, 512, 1024)
+        bias(0, 512, 1024, range(1))
+        unbound(3, *snd)
         s_quant(2)
+        product(3, *fst)
+        bias(0, 512, 1024, range(1, 4))
+        store(0, 512, 1024)
         readout(1, 0, range(4), range(2))
+        product(3, *snd)
         o_cast(0, 0, 512, True)
         o_cast(0, 512, 1024, True)
-        product(3, 0, 256)
-        product(3, 256, 512)
         s_quant(3, 0, 256)
         s_quant(3, 256, 512)
         readout(1, 1, range(4), range(2))
         o_quant(0, 0, 512)
+        bias(1, 0, 512, range(2))
         o_quant(0, 512, 1024)
         store_scales(0, 0, 1024)
-        bias(1, 0, 512, range(4))
+        bias(1, 0, 512, range(2, 4))
         store(1, 0, 512)
         o_cast(1, 0, 512, True)
-        for t in range(4):
-            bias(1, 512, 1024, [t])
-            store(1, 512, 1024, slice(t, t + 1))
+        bias(1, 512, 1024, range(2))
+        store(1, 512, 1024, slice(0, 2))
+        bias(1, 512, 1024, range(2, 4))
+        store(1, 512, 1024, slice(2, 4))
         o_quant(1, 0, 512)
         o_cast(1, 512, 768, False)
         o_cast(1, 768, 1024, True)

@@ -18,6 +18,7 @@ MULT = mybir.AluOpType.mult
 ACT = mybir.ActivationFunctionType
 
 P = 128
+WARM = 4
 KAPPA = 0.8125
 
 
@@ -26,7 +27,7 @@ def tile_twostrandmotifboltzmannoccupancyreadout_x1_kernel(tc, xf, xr, w, mu, a,
     with ExitStack() as ctx:
         keep = ctx.enter_context(tc.tile_pool(name="keep", bufs=1))
         ring = ctx.enter_context(tc.tile_pool(name="ring", bufs=7))
-        epool = ctx.enter_context(tc.tile_pool(name="epool", bufs=2))
+        epool = ctx.enter_context(tc.tile_pool(name="epool", bufs=3))
         psum = ctx.enter_context(tc.psum_pool(name="psum", bufs=8))
         ctx.enter_context(tc.manual_schedule())
 
@@ -41,6 +42,7 @@ def tile_twostrandmotifboltzmannoccupancyreadout_x1_kernel(tc, xf, xr, w, mu, a,
         mu_raw = kt([P, 8], BF16, "mu_raw")
         a_raw = kt([P, 8], BF16, "a_raw")
         mu_f = kt([P, 8], F32, "mu_f")
+        table = kt([P, 1], F32, "table")
         a_neg = kt([P, 8], F32, "a_neg")
         b_all = kt([P, T], BF16, "b_all")
 
@@ -62,42 +64,56 @@ def tile_twostrandmotifboltzmannoccupancyreadout_x1_kernel(tc, xf, xr, w, mu, a,
         o_codes = [kt([P, T], U32, "o_codes%d" % h) for h in range(2)]
         o_scales = [kt([P, T], U8, "o_scales%d" % h) for h in range(2)]
 
-        nc.scalar.dma_start(out=mu_raw[:].rearrange("p (g t) -> p g t", t=4), in_=mu.rearrange("(g p t) -> p g t", p=P, t=4))
-        nc.scalar.dma_start(out=a_raw[:].rearrange("p (g t) -> p g t", t=4), in_=a.rearrange("(g p t) -> p g t", p=P, t=4))
+        def load_w(g, lo, hi):
+            nc.sync.dma_start(
+                out=w_raw[g][:, :, lo:hi],
+                in_=w[:, 512 * g + lo : 512 * g + hi].rearrange("(p j) c -> p j c", j=4),
+            )
 
-        def load_w(g):
-            nc.sync.dma_start(out=w_raw[g][:], in_=w[:, 512 * g : 512 * g + 512].rearrange("(p j) c -> p j c", j=4))
-
-        def load_x(s, h):
+        def load_x(s, h, slots):
             src = (xf, xr)[s]
-            nc.sync.dma_start(out=x_raw[s, h][:], in_=src[512 * h : 512 * h + 512, :].rearrange("(p t) k -> p t k", t=4))
+            nc.sync.dma_start(
+                out=x_raw[s, h][:, slots, :],
+                in_=src[512 * h : 512 * h + 512, :].rearrange("(p t) k -> p t k", t=4)[:, slots, :],
+            )
 
         def load_r(g):
             nc.sync.dma_start(out=r_raw[g][:], in_=r[512 * g : 512 * g + 512, :].rearrange("(p j) c -> p j c", j=4))
 
-        load_w(0)
-        load_x(0, 0)
-        load_w(1)
-        load_x(1, 0)
+        low, high, whole = slice(0, 2), slice(2, 4), slice(0, 4)
+        load_w(0, 0, 256)
+        load_w(0, 256, 512)
+        load_x(0, 0, low)
+        load_x(0, 0, high)
+        load_x(1, 0, low)
+        load_x(1, 0, high)
+        nc.sync.dma_start(out=mu_raw[:].rearrange("p (g t) -> p g t", t=4), in_=mu.rearrange("(g p t) -> p g t", p=P, t=4))
+        load_w(1, 0, 512)
         load_r(0)
-        load_x(0, 1)
-        load_x(1, 1)
+        load_x(0, 1, whole)
+        load_x(1, 1, whole)
         load_r(1)
+        nc.sync.dma_start(out=a_raw[:].rearrange("p (g t) -> p g t", t=4), in_=a.rearrange("(g p t) -> p g t", p=P, t=4))
         nc.sync.dma_start(out=b_all[:], in_=b.partition_broadcast(P))
 
-        nc.scalar.copy(out=mu_f[:], in_=mu_raw[:])
-        nc.scalar.mul(out=a_neg[:], in_=a_raw[:], mul=-KAPPA)
+        warm = kt([P, 512], BF16, "warm")
+        nc.vector.memset(warm[:], 0.0)
+        for i in range(WARM):
+            bank = psum.tile([P, 512], F32, name="bank")
+            nc.tensor.matmul(bank[:], warm[:, 0:P], warm[:], start=True, stop=True)
+        nc.scalar.copy(out=table[:], in_=warm[:, 0:1])
 
         def quantize(codes, scales, rows):
             nc.vector.quantize_mx(out=codes.bitcast(FP8X4), scales=scales, in_=rows.rearrange("p c j -> p (c j)"))
 
         box = {}
 
-        def w_copy(g):
-            box["w", g] = grouped()
+        def w_copy(g, lo, hi):
+            if lo == 0:
+                box["w", g] = grouped()
             nc.vector.tensor_copy(
-                out=box["w", g][:].rearrange("p (t m) j -> p t m j", t=4),
-                in_=w_raw[g][:].rearrange("p j (m t) -> p t m j", t=4),
+                out=box["w", g][:].rearrange("p (t m) j -> p t m j", t=4)[:, :, lo // 4 : hi // 4, :],
+                in_=w_raw[g][:, :, lo:hi].rearrange("p j (m t) -> p t m j", t=4),
             )
 
         def w_quant(g):
@@ -244,59 +260,64 @@ def tile_twostrandmotifboltzmannoccupancyreadout_x1_kernel(tc, xf, xr, w, mu, a,
 
         on_act = nc.scalar.copy
         on_vec = nc.vector.tensor_copy
-        w_copy(0)
+        fst, snd = (0, 256), (256, 512)
+        w_copy(0, *fst)
+        w_copy(0, *snd)
         x_turn(0, 0, on_act)
         w_quant(0)
-        w_copy(1)
-        x_turn(1, 0, on_act)
         x_quant(0, 0)
-        w_quant(1)
+        x_turn(1, 0, on_act)
+        nc.scalar.copy(out=mu_f[:], in_=mu_raw[:])
         scores(0, [0])
         scores(1, [0])
+        w_copy(1, *fst)
         x_quant(1, 0)
         scores(0, [1])
         scores(1, [1])
+        w_copy(1, *snd)
         extra = {
-            2: [lambda: r_copy(0, 0)],
-            3: [lambda: r_copy(0, 1), lambda: x_turn(0, 1, on_vec), lambda: x_turn(1, 1, on_vec)],
-            4: [lambda: add_parts(0, 0, 256), lambda: x_quant(0, 1)],
-            5: [lambda: add_parts(0, 256, 512), lambda: x_quant(1, 1)],
-            6: [lambda: r_quant(0, 0)],
-            7: [lambda: r_quant(0, 1)],
-            8: [lambda: r_copy(1, 0), lambda: add_parts(1, 0, 256)],
-            9: [lambda: add_parts(1, 256, 512), lambda: r_quant(1, 0)],
-            10: [lambda: r_copy(1, 1)],
-            12: [lambda: add_parts(2, 0, 256)],
+            2: [lambda: w_quant(1), lambda: r_copy(0, 0)],
+            3: [lambda: x_turn(0, 1, on_vec)],
+            4: [lambda: x_turn(1, 1, on_vec), lambda: x_quant(0, 1), lambda: add_parts(0, 0, 256), lambda: x_quant(1, 1)],
+            5: [lambda: add_parts(0, 256, 512), lambda: r_quant(0, 0)],
+            6: [lambda: r_copy(0, 1)],
+            8: [lambda: add_parts(1, 0, 256), lambda: r_quant(0, 1)],
+            9: [lambda: add_parts(1, 256, 512)],
+            10: [lambda: r_copy(1, 0)],
+            12: [lambda: add_parts(2, 0, 256), lambda: r_quant(1, 0)],
             13: [lambda: add_parts(2, 256, 512)],
         }
         for i in range(2, 16):
             scores(i)
             for job in extra.get(i, []):
                 job()
-        fst, snd = (0, 256), (256, 512)
+        nc.scalar.mul(out=a_neg[:], in_=a_raw[:], mul=-KAPPA)
         add_parts(3, *fst)
-        add_parts(3, *snd)
-        r_quant(1, 1)
         root(0, *fst)
         root(0, *snd)
+        add_parts(3, *snd)
         unbound_v(0, *fst)
         unbound(0, *snd)
         product(0, *fst)
         root(1, *fst)
         root(1, *snd)
-        unbound(1, *fst)
         product(0, *snd)
+        unbound(1, *fst)
+        r_copy(1, 1)
         root(2, *fst)
         unbound(1, *snd)
         s_quant(0)
-        readout(0, 0, range(4), range(2))
+        readout(0, 0, range(4), [0])
         product(1, *fst)
+        r_quant(1, 1)
         root(2, *snd)
         unbound(2, *fst)
         product(1, *snd)
         root(3, *fst)
         s_quant(1)
-        readout(0, 1, range(4), range(2))
+        readout(0, 1, range(4), [0])
+        readout(0, 0, range(4), [1])
+        readout(0, 1, range(4), [1])
         unbound(2, *snd)
         product(2, *fst)
         bias(0, 0, 512, range(3))
@@ -305,33 +326,35 @@ def tile_twostrandmotifboltzmannoccupancyreadout_x1_kernel(tc, xf, xr, w, mu, a,
         product(2, *snd)
         bias(0, 0, 512, range(3, 4))
         store(0, 0, 512)
-        bias(0, 512, 1024, range(1))
         unbound(3, *snd)
+        o_cast(0, 0, 512, True)
+        bias(0, 512, 1024, range(1))
         s_quant(2)
         product(3, *fst)
         bias(0, 512, 1024, range(1, 4))
         store(0, 512, 1024)
+        o_cast(0, 512, 1024, True)
         readout(1, 0, range(4), range(2))
         product(3, *snd)
-        o_cast(0, 0, 512, True)
-        o_cast(0, 512, 1024, True)
         s_quant(3, 0, 256)
         s_quant(3, 256, 512)
         readout(1, 1, range(4), range(2))
-        o_quant(0, 0, 512)
-        bias(1, 0, 512, range(2))
+        for t in range(4):
+            bias(1, 0, 512, [t])
+            store(1, 0, 512, slice(t, t + 1))
+            if t == 1:
+                o_quant(0, 0, 512)
+        o_cast(1, 0, 512, True)
         o_quant(0, 512, 1024)
         store_scales(0, 0, 1024)
-        bias(1, 0, 512, range(2, 4))
-        store(1, 0, 512)
-        o_cast(1, 0, 512, True)
-        bias(1, 512, 1024, range(2))
-        store(1, 512, 1024, slice(0, 2))
-        bias(1, 512, 1024, range(2, 4))
-        store(1, 512, 1024, slice(2, 4))
+        bias(1, 512, 768, range(4))
+        store(1, 512, 768)
+        o_cast(1, 512, 768, True)
+        bias(1, 768, 1024, range(4))
+        store(1, 768, 1024)
         o_quant(1, 0, 512)
-        o_cast(1, 512, 768, False)
-        o_cast(1, 768, 1024, True)
         o_quant(1, 512, 768)
+        o_cast(1, 768, 896, False)
+        o_cast(1, 896, 1024, True)
         o_quant(1, 768, 1024)
         store_scales(1, 0, 1024)

@@ -19,6 +19,7 @@ ACT = mybir.ActivationFunctionType
 
 P = 128
 WARM = 4
+PIECES = (((0, 512), (512, 1024)), ((0, 512), (512, 768), (768, 1024)))
 KAPPA = 0.8125
 
 
@@ -46,7 +47,7 @@ def tile_twostrandmotifboltzmannoccupancyreadout_x1_kernel(tc, xf, xr, w, mu, a,
         a_neg = kt([P, 8], F32, "a_neg")
         b_all = kt([P, T], BF16, "b_all")
 
-        w_raw = [kt([P, 4, 512], BF16, "w_raw%d" % g) for g in range(2)]
+        w_raw = {(g, n): kt([P, 4, 256], BF16, "w_raw%d%d" % (g, n)) for g in range(2) for n in range(2)}
         w_codes = [kt([P, 512], U32, "w_codes%d" % g) for g in range(2)]
         w_scales = [kt([P, 512], U8, "w_scales%d" % g) for g in range(2)]
         x_raw = {(s, h): kt([P, 4, 512], BF16, "x_raw%d%d" % (s, h)) for s in range(2) for h in range(2)}
@@ -60,13 +61,13 @@ def tile_twostrandmotifboltzmannoccupancyreadout_x1_kernel(tc, xf, xr, w, mu, a,
         nc.gpsimd.memset(kappa[:], KAPPA)
         s_codes = [kt([P, 512], U32, "s_codes%d" % k) for k in range(4)]
         s_scales = [kt([P, 512], U8, "s_scales%d" % k) for k in range(4)]
-        o_f32 = [kt([P, 4, T], F32, "o_f32%d" % h) for h in range(2)]
+        o_f32 = {(h, lo): kt([P, 4, hi - lo], F32, "o_f32%d%d" % (h, lo)) for h in range(2) for lo, hi in PIECES[h]}
         o_codes = [kt([P, T], U32, "o_codes%d" % h) for h in range(2)]
         o_scales = [kt([P, T], U8, "o_scales%d" % h) for h in range(2)]
 
         def load_w(g, lo, hi):
             nc.sync.dma_start(
-                out=w_raw[g][:, :, lo:hi],
+                out=w_raw[g, lo // 256][:],
                 in_=w[:, 512 * g + lo : 512 * g + hi].rearrange("(p j) c -> p j c", j=4),
             )
 
@@ -88,7 +89,8 @@ def tile_twostrandmotifboltzmannoccupancyreadout_x1_kernel(tc, xf, xr, w, mu, a,
         load_x(1, 0, low)
         load_x(1, 0, high)
         nc.sync.dma_start(out=mu_raw[:].rearrange("p (g t) -> p g t", t=4), in_=mu.rearrange("(g p t) -> p g t", p=P, t=4))
-        load_w(1, 0, 512)
+        load_w(1, 0, 256)
+        load_w(1, 256, 512)
         load_r(0)
         load_x(0, 1, whole)
         load_x(1, 1, whole)
@@ -113,7 +115,7 @@ def tile_twostrandmotifboltzmannoccupancyreadout_x1_kernel(tc, xf, xr, w, mu, a,
                 box["w", g] = grouped()
             nc.vector.tensor_copy(
                 out=box["w", g][:].rearrange("p (t m) j -> p t m j", t=4)[:, :, lo // 4 : hi // 4, :],
-                in_=w_raw[g][:, :, lo:hi].rearrange("p j (m t) -> p t m j", t=4),
+                in_=w_raw[g, lo // 256][:].rearrange("p j (m t) -> p t m j", t=4),
             )
 
         def w_quant(g):
@@ -223,20 +225,20 @@ def tile_twostrandmotifboltzmannoccupancyreadout_x1_kernel(tc, xf, xr, w, mu, a,
         def bias(h, lo, hi, slices):
             n = lo // 512
             for t in slices:
-                nc.vector.tensor_tensor(out=o_f32[h][:, t, lo:hi], in0=box["o", h, n, t][:, lo - 512 * n : hi - 512 * n], in1=b_all[:, lo:hi], op=ADD)
+                nc.vector.tensor_tensor(out=o_f32[h, lo][:, t, :], in0=box["o", h, n, t][:, lo - 512 * n : hi - 512 * n], in1=b_all[:, lo:hi], op=ADD)
 
         def store(h, lo, hi, slices=slice(0, 4)):
             nc.sync.dma_start(
                 out=out_0[512 * h : 512 * h + 512, lo:hi].rearrange("(p t) c -> p t c", t=4)[:, slices, :],
-                in_=o_f32[h][:, slices, lo:hi],
+                in_=o_f32[h, lo][:, slices, :],
             )
 
-        def o_cast(h, lo, hi, on_act):
+        def o_cast(h, piece, lo, hi, on_act):
             n = lo // 512
             if lo == 512 * n:
                 box["og", h, n] = grouped()
             dst = box["og", h, n][:, lo - 512 * n : hi - 512 * n, :].rearrange("p (c i) t -> p c t i", i=4)
-            src = o_f32[h][:, :, lo:hi].rearrange("p t (c i) -> p c t i", i=4)
+            src = o_f32[h, piece][:, :, lo - piece : hi - piece].rearrange("p t (c i) -> p c t i", i=4)
             if on_act:
                 nc.scalar.copy(out=dst, in_=src)
             else:
@@ -327,13 +329,13 @@ def tile_twostrandmotifboltzmannoccupancyreadout_x1_kernel(tc, xf, xr, w, mu, a,
         bias(0, 0, 512, range(3, 4))
         store(0, 0, 512)
         unbound(3, *snd)
-        o_cast(0, 0, 512, True)
+        o_cast(0, 0, 0, 512, True)
         bias(0, 512, 1024, range(1))
         s_quant(2)
         product(3, *fst)
         bias(0, 512, 1024, range(1, 4))
         store(0, 512, 1024)
-        o_cast(0, 512, 1024, True)
+        o_cast(0, 512, 512, 1024, True)
         readout(1, 0, range(4), range(2))
         product(3, *snd)
         s_quant(3, 0, 256)
@@ -344,17 +346,17 @@ def tile_twostrandmotifboltzmannoccupancyreadout_x1_kernel(tc, xf, xr, w, mu, a,
             store(1, 0, 512, slice(t, t + 1))
             if t == 1:
                 o_quant(0, 0, 512)
-        o_cast(1, 0, 512, True)
+        o_cast(1, 0, 0, 512, True)
         o_quant(0, 512, 1024)
         store_scales(0, 0, 1024)
         bias(1, 512, 768, range(4))
         store(1, 512, 768)
-        o_cast(1, 512, 768, True)
+        o_cast(1, 512, 512, 768, True)
         bias(1, 768, 1024, range(4))
         store(1, 768, 1024)
         o_quant(1, 0, 512)
         o_quant(1, 512, 768)
-        o_cast(1, 768, 896, False)
-        o_cast(1, 896, 1024, True)
+        o_cast(1, 768, 768, 896, False)
+        o_cast(1, 768, 896, 1024, True)
         o_quant(1, 768, 1024)
         store_scales(1, 0, 1024)

@@ -227,6 +227,13 @@ def tile_twostrandmotifboltzmannoccupancyreadout_x1_kernel(tc, xf, xr, w, mu, a,
             for t in slices:
                 nc.vector.tensor_tensor(out=o_f32[h, lo][:, t, :], in0=box["o", h, n, t][:, lo - 512 * n : hi - 512 * n], in1=b_all[:, lo:hi], op=ADD)
 
+        def bias_two_steps(h, lo, hi, slices):
+            n = lo // 512
+            for t in slices:
+                part = o_f32[h, lo][:, t, :]
+                nc.scalar.copy(out=part, in_=box["o", h, n, t][:, lo - 512 * n : hi - 512 * n])
+                nc.gpsimd.tensor_tensor(out=part, in0=part, in1=b_all[:, lo:hi], op=ADD)
+
         def store(h, lo, hi, slices=slice(0, 4)):
             nc.sync.dma_start(
                 out=out_0[512 * h : 512 * h + 512, lo:hi].rearrange("(p t) c -> p t c", t=4)[:, slices, :],
@@ -329,34 +336,35 @@ def tile_twostrandmotifboltzmannoccupancyreadout_x1_kernel(tc, xf, xr, w, mu, a,
         bias(0, 0, 512, range(3, 4))
         store(0, 0, 512)
         unbound(3, *snd)
+        bias_two_steps(0, 512, 1024, [3])
         o_cast(0, 0, 0, 512, True)
         bias(0, 512, 1024, range(1))
         s_quant(2)
         product(3, *fst)
-        bias(0, 512, 1024, range(1, 4))
+        bias(0, 512, 1024, range(1, 3))
         store(0, 512, 1024)
         o_cast(0, 512, 512, 1024, True)
         readout(1, 0, range(4), range(2))
         product(3, *snd)
         s_quant(3, 0, 256)
         s_quant(3, 256, 512)
-        readout(1, 1, range(4), range(2))
-        for t in range(4):
+        readout(1, 1, [3, 0, 1, 2], [0])
+        readout(1, 1, range(4), [1])
+        bias_two_steps(1, 0, 512, [3])
+        o_quant(0, 0, 512)
+        for t in range(3):
             bias(1, 0, 512, [t])
             store(1, 0, 512, slice(t, t + 1))
-            if t == 1:
-                o_quant(0, 0, 512)
-        o_cast(1, 0, 0, 512, True)
-        o_quant(0, 512, 1024)
-        store_scales(0, 0, 1024)
         bias(1, 512, 768, range(4))
+        store(1, 0, 512, slice(3, 4))
+        o_cast(1, 0, 0, 512, True)
         store(1, 512, 768)
         o_cast(1, 512, 512, 768, True)
         bias(1, 768, 1024, range(4))
         store(1, 768, 1024)
+        o_quant(0, 512, 1024)
+        store_scales(0, 0, 1024)
         o_quant(1, 0, 512)
-        o_quant(1, 512, 768)
-        o_cast(1, 768, 768, 896, False)
-        o_cast(1, 768, 896, 1024, True)
-        o_quant(1, 768, 1024)
+        o_cast(1, 768, 768, 1024, False)
+        o_quant(1, 512, 1024)
         store_scales(1, 0, 1024)

from contextlib import ExitStack

import concourse.mybir as mybir
from concourse.masks import make_identity

B, K, M, T = 1024, 512, 1024, 1024
FLOPS = 2 * (2 * B * K * M) + 2 * B * M * T

F32 = mybir.dt.float32
BF16 = mybir.dt.bfloat16
U32 = mybir.dt.uint32
I32 = mybir.dt.int32
U8 = mybir.dt.uint8
FP8X4 = mybir.dt.float8_e4m3fn_x4
ADD = mybir.AluOpType.add
SUB = mybir.AluOpType.subtract
MULT = mybir.AluOpType.mult
ACT = mybir.ActivationFunctionType

P = 128
WARM = 4
PIECES = (((0, 512), (512, 1024)), ((0, 512), (512, 768), (768, 1024)))
KAPPA = 0.8125


def tile_twostrandmotifboltzmannoccupancyreadout_x1_kernel(tc, xf, xr, w, mu, a, r, b, out_0, out_1, out_2):
    nc = tc.nc
    with ExitStack() as ctx:
        keep = ctx.enter_context(tc.tile_pool(name="keep", bufs=1))
        ring = ctx.enter_context(tc.tile_pool(name="ring", bufs=7))
        epool = ctx.enter_context(tc.tile_pool(name="epool", bufs=3))
        psum = ctx.enter_context(tc.psum_pool(name="psum", bufs=8))
        ctx.enter_context(tc.manual_schedule())

        def kt(shape, dtype, name):
            return keep.tile(shape, dtype, name=name, align_bytes=64)

        def grouped():
            return ring.tile([P, 512, 4], BF16, name="grouped", align_bytes=64)

        ident = kt([P, P], F32, "ident")
        make_identity(nc, ident[:])
        mu_raw = kt([P, 8], BF16, "mu_raw")
        a_raw = kt([P, 8], BF16, "a_raw")
        mu_f = kt([P, 8], F32, "mu_f")
        table = kt([P, 1], F32, "table")
        a_neg = kt([P, 8], F32, "a_neg")
        b_all = kt([P, T], BF16, "b_all")

        w_raw = {(g, n): kt([P, 4, 256], BF16, "w_raw%d%d" % (g, n)) for g in range(2) for n in range(2)}
        w_codes = [kt([P, 512], U32, "w_codes%d" % g) for g in range(2)]
        w_scales = [kt([P, 512], U8, "w_scales%d" % g) for g in range(2)]
        x_raw = {(s, h): kt([P, 4, 512], BF16, "x_raw%d%d" % (s, h)) for s in range(2) for h in range(2)}
        x_codes = {(s, h): kt([P, 512], U32, "x_codes%d%d" % (s, h)) for s in range(2) for h in range(2)}
        x_scales = {(s, h): kt([P, 512], U8, "x_scales%d%d" % (s, h)) for s in range(2) for h in range(2)}
        r_raw = [kt([P, 4, T], BF16, "r_raw%d" % g) for g in range(2)]
        r_codes = [kt([P, T], U32, "r_codes%d" % g) for g in range(2)]
        r_scales = [kt([P, T], U8, "r_scales%d" % g) for g in range(2)]
        weight = [kt([P, 512, 4], F32, "weight%d" % k) for k in range(4)]
        kappa = kt([P, 1], F32, "kappa")
        nc.gpsimd.memset(kappa[:], KAPPA)
        s_codes = [kt([P, 512], U32, "s_codes%d" % k) for k in range(4)]
        s_scales = [kt([P, 512], U8, "s_scales%d" % k) for k in range(4)]
        o_f32 = {(h, lo): kt([P, 4, hi - lo], F32, "o_f32%d%d" % (h, lo)) for h in range(2) for lo, hi in PIECES[h]}
        o_codes = [kt([P, T], U32, "o_codes%d" % h) for h in range(2)]
        o_scales = [kt([P, T], U8, "o_scales%d" % h) for h in range(2)]

        def load_w(g, lo, hi):
            nc.sync.dma_start(
                out=w_raw[g, lo // 256][:],
                in_=w[:, 512 * g + lo : 512 * g + hi].rearrange("(p j) c -> p j c", j=4),
            )

        def load_x(s, h, slots):
            src = (xf, xr)[s]
            nc.sync.dma_start(
                out=x_raw[s, h][:, slots, :],
                in_=src[512 * h : 512 * h + 512, :].rearrange("(p t) k -> p t k", t=4)[:, slots, :],
            )

        def load_r(g):
            nc.sync.dma_start(out=r_raw[g][:], in_=r[512 * g : 512 * g + 512, :].rearrange("(p j) c -> p j c", j=4))

        low, high, whole = slice(0, 2), slice(2, 4), slice(0, 4)
        load_w(0, 0, 256)
        load_w(0, 256, 512)
        load_x(0, 0, low)
        load_x(0, 0, high)
        load_x(1, 0, low)
        load_x(1, 0, high)
        nc.sync.dma_start(out=mu_raw[:].rearrange("p (g t) -> p g t", t=4), in_=mu.rearrange("(g p t) -> p g t", p=P, t=4))
        load_w(1, 0, 256)
        load_w(1, 256, 512)
        load_r(0)
        load_x(0, 1, whole)
        load_x(1, 1, whole)
        load_r(1)
        nc.sync.dma_start(out=a_raw[:].rearrange("p (g t) -> p g t", t=4), in_=a.rearrange("(g p t) -> p g t", p=P, t=4))
        nc.sync.dma_start(out=b_all[:], in_=b.partition_broadcast(P))

        warm = kt([P, 512], BF16, "warm")
        nc.vector.memset(warm[:], 0.0)
        for i in range(WARM):
            bank = psum.tile([P, 512], F32, name="bank")
            nc.tensor.matmul(bank[:], warm[:, 0:P], warm[:], start=True, stop=True)
        nc.scalar.copy(out=table[:], in_=warm[:, 0:1])

        def quantize(codes, scales, rows):
            nc.vector.quantize_mx(out=codes.bitcast(FP8X4), scales=scales, in_=rows.rearrange("p c j -> p (c j)"))

        box = {}

        def w_copy(g, lo, hi):
            if lo == 0:
                box["w", g] = grouped()
            nc.vector.tensor_copy(
                out=box["w", g][:].rearrange("p (t m) j -> p t m j", t=4)[:, :, lo // 4 : hi // 4, :],
                in_=w_raw[g, lo // 256][:].rearrange("p j (m t) -> p t m j", t=4),
            )

        def w_quant(g):
            quantize(w_codes[g][:], w_scales[g][:], box["w", g][:])

        def r_copy(g, n):
            box["r", g, n] = grouped()
            nc.vector.tensor_copy(
                out=box["r", g, n][:].rearrange("p (c i) j -> p c j i", i=4),
                in_=r_raw[g][:, :, 512 * n : 512 * n + 512].rearrange("p j (c i) -> p c j i", i=4),
            )

        def r_quant(g, n):
            cols = slice(512 * n, 512 * n + 512)
            quantize(r_codes[g][:, cols], r_scales[g][:, cols], box["r", g, n][:])

        def x_turn(s, h, copy, halves=range(2)):
            words = x_raw[s, h][:].bitcast(F32)
            if 0 in halves:
                box["x", s, h] = grouped()
            for half in halves:
                bank = psum.tile([P, 2, 2, P], F32, name="bank")
                for q in range(2):
                    for u in range(2):
                        nc.tensor.transpose(bank[:, q, u, :], words[:, 2 * half + q, u::2], ident[:])
                copy(
                    out=box["x", s, h][:, 256 * half : 256 * half + 256, :].bitcast(F32).rearrange("p (q n) u -> p q n u", q=2),
                    in_=bank[:].rearrange("p q u n -> p q n u"),
                )

        def x_quant(s, h):
            quantize(x_codes[s, h][:], x_scales[s, h][:], box["x", s, h][:])

        def scores(i, strands=range(2)):
            h, m = divmod(i, 8)
            g, t = divmod(m, 4)
            cols = slice(P * t, P * t + P)
            for s in strands:
                bank = psum.tile([P, 512], F32, name="bank")
                nc.tensor.matmul_mx(
                    out=bank[:],
                    lhsT=w_codes[g][:, cols].bitcast(FP8X4),
                    lhsT_scale=w_scales[g][:, cols],
                    rhs=x_codes[s, h][:].bitcast(FP8X4),
                    rhs_scale=x_scales[s, h][:],
                    start=True,
                    stop=True,
                )
                if t == 0:
                    box["e", i // 4, s] = epool.tile([P, 4, 512], F32, name="e%d" % s)
                nc.scalar.activation(out=box["e", i // 4, s][:, t, :], in_=bank[:], func=ACT.Exp, bias=mu_f[:, m : m + 1])

        def add_parts(k, lo, hi):
            parts = [box["e", k, s][:, :, lo:hi].rearrange("p t (c i) -> p c t i", i=4) for s in range(2)]
            nc.vector.tensor_tensor(
                out=weight[k][:, lo:hi, :].rearrange("p (c i) t -> p c t i", i=4),
                in0=parts[0],
                in1=parts[1],
                op=ADD,
            )

        def root(k, lo, hi):
            part = weight[k][:, lo:hi, :].rearrange("p c t -> p (c t)")
            nc.scalar.activation(out=part, in_=part, func=ACT.Abs_reciprocal_sqrt, scale=KAPPA, bias=kappa[:])

        def unbound(k, lo, hi):
            part = weight[k][:, lo:hi, :].rearrange("p c t -> p (c t)")
            nc.scalar.activation(out=part, in_=part, func=ACT.Square)

        def unbound_v(k, lo, hi):
            part = weight[k][:, lo:hi, :].rearrange("p c t -> p (c t)")
            nc.vector.tensor_tensor(out=part, in0=part, in1=part, op=MULT)

        def product(k, lo, hi):
            if lo == 0:
                box["s", k] = grouped()
            g = k % 2
            nc.vector.scalar_tensor_tensor(
                out=box["s", k][:, lo:hi, :],
                in0=weight[k][:, lo:hi, :],
                scalar=0.5 / KAPPA,
                in1=a_neg[:, 4 * g : 4 * g + 4].unsqueeze(1).to_broadcast([P, hi - lo, 4]),
                op0=SUB,
                op1=MULT,
            )

        def s_quant(k, lo=0, hi=512):
            quantize(s_codes[k][:, lo:hi], s_scales[k][:, lo:hi], box["s", k][:, lo:hi, :])

        def readout(h, g, slices, blocks):
            for n in blocks:
                for t in slices:
                    if g == 0:
                        box["o", h, n, t] = psum.tile([P, 512], F32, name="bank")
                    cols = slice(512 * n, 512 * n + 512)
                    rows = slice(P * t, P * t + P)
                    nc.tensor.matmul_mx(
                        out=box["o", h, n, t][:],
                        lhsT=s_codes[2 * h + g][:, rows].bitcast(FP8X4),
                        lhsT_scale=s_scales[2 * h + g][:, rows],
                        rhs=r_codes[g][:, cols].bitcast(FP8X4),
                        rhs_scale=r_scales[g][:, cols],
                        start=(g == 0),
                        stop=(g == 1),
                    )

        def bias(h, lo, hi, slices):
            n = lo // 512
            for t in slices:
                nc.vector.tensor_tensor(out=o_f32[h, lo][:, t, :], in0=box["o", h, n, t][:, lo - 512 * n : hi - 512 * n], in1=b_all[:, lo:hi], op=ADD)

        def bias_two_steps(h, lo, hi, slices):
            n = lo // 512
            for t in slices:
                part = o_f32[h, lo][:, t, :]
                nc.scalar.copy(out=part, in_=box["o", h, n, t][:, lo - 512 * n : hi - 512 * n])
                nc.gpsimd.tensor_tensor(out=part, in0=part, in1=b_all[:, lo:hi], op=ADD)

        def store(h, lo, hi, slices=slice(0, 4)):
            nc.sync.dma_start(
                out=out_0[512 * h : 512 * h + 512, lo:hi].rearrange("(p t) c -> p t c", t=4)[:, slices, :],
                in_=o_f32[h, lo][:, slices, :],
            )

        def o_cast(h, piece, lo, hi, on_act):
            n = lo // 512
            if lo == 512 * n:
                box["og", h, n] = grouped()
            dst = box["og", h, n][:, lo - 512 * n : hi - 512 * n, :].rearrange("p (c i) t -> p c t i", i=4)
            src = o_f32[h, piece][:, :, lo - piece : hi - piece].rearrange("p t (c i) -> p c t i", i=4)
            if on_act:
                nc.scalar.copy(out=dst, in_=src)
            else:
                nc.vector.tensor_copy(out=dst, in_=src)

        def o_quant(h, lo, hi):
            n = lo // 512
            cols = slice(lo, hi)
            quantize(o_codes[h][:, cols], o_scales[h][:, cols], box["og", h, n][:, lo - 512 * n : hi - 512 * n, :])
            nc.sync.dma_start(
                out=out_1[h, :, cols, :].rearrange("p c t -> p (c t)").bitcast(I32),
                in_=o_codes[h][:, cols].bitcast(I32),
            )

        def store_scales(h, lo, hi):
            for q in range(4):
                nc.sync.dma_start(
                    out=out_2[h, 4 * q : 4 * q + 4, lo:hi].bitcast(I32),
                    in_=o_scales[h][32 * q : 32 * q + 4, lo:hi].bitcast(I32),
                )

        on_act = nc.scalar.copy
        on_vec = nc.vector.tensor_copy
        fst, snd = (0, 256), (256, 512)
        w_copy(0, *fst)
        w_copy(0, *snd)
        x_turn(0, 0, on_act)
        w_quant(0)
        x_quant(0, 0)
        x_turn(1, 0, on_act)
        nc.scalar.copy(out=mu_f[:], in_=mu_raw[:])
        scores(0, [0])
        scores(1, [0])
        w_copy(1, *fst)
        x_quant(1, 0)
        scores(0, [1])
        scores(1, [1])
        w_copy(1, *snd)
        extra = {
            2: [lambda: w_quant(1), lambda: r_copy(0, 0)],
            3: [lambda: x_turn(0, 1, on_vec)],
            4: [lambda: x_turn(1, 1, on_vec), lambda: x_quant(0, 1), lambda: add_parts(0, 0, 256), lambda: x_quant(1, 1)],
            5: [lambda: add_parts(0, 256, 512), lambda: r_quant(0, 0)],
            6: [lambda: r_copy(0, 1)],
            8: [lambda: add_parts(1, 0, 256), lambda: r_quant(0, 1)],
            9: [lambda: add_parts(1, 256, 512)],
            10: [lambda: r_copy(1, 0)],
            12: [lambda: add_parts(2, 0, 256), lambda: r_quant(1, 0)],
            13: [lambda: add_parts(2, 256, 512)],
        }
        for i in range(2, 16):
            scores(i)
            for job in extra.get(i, []):
                job()
        nc.scalar.mul(out=a_neg[:], in_=a_raw[:], mul=-KAPPA)
        add_parts(3, *fst)
        root(0, *fst)
        root(0, *snd)
        add_parts(3, *snd)
        unbound_v(0, *fst)
        unbound(0, *snd)
        product(0, *fst)
        root(1, *fst)
        root(1, *snd)
        product(0, *snd)
        unbound(1, *fst)
        r_copy(1, 1)
        root(2, *fst)
        unbound(1, *snd)
        s_quant(0)
        readout(0, 0, range(4), [0])
        product(1, *fst)
        r_quant(1, 1)
        root(2, *snd)
        unbound(2, *fst)
        product(1, *snd)
        root(3, *fst)
        s_quant(1)
        readout(0, 1, range(4), [0])
        readout(0, 0, range(4), [1])
        readout(0, 1, range(4), [1])
        unbound(2, *snd)
        product(2, *fst)
        bias(0, 0, 512, range(3))
        root(3, *snd)
        unbound(3, *fst)
        product(2, *snd)
        bias(0, 0, 512, range(3, 4))
        store(0, 0, 512)
        unbound(3, *snd)
        bias_two_steps(0, 512, 1024, [3])
        o_cast(0, 0, 0, 512, True)
        bias(0, 512, 1024, range(1))
        s_quant(2)
        product(3, *fst)
        bias(0, 512, 1024, range(1, 3))
        store(0, 512, 1024)
        o_cast(0, 512, 512, 1024, True)
        readout(1, 0, range(4), range(2))
        product(3, *snd)
        s_quant(3, 0, 256)
        s_quant(3, 256, 512)
        readout(1, 1, [3, 0, 1, 2], [0])
        readout(1, 1, range(4), [1])
        bias_two_steps(1, 0, 512, [3])
        o_quant(0, 0, 512)
        for t in range(3):
            bias(1, 0, 512, [t])
            store(1, 0, 512, slice(t, t + 1))
        bias(1, 512, 768, range(4))
        store(1, 0, 512, slice(3, 4))
        o_cast(1, 0, 0, 512, True)
        store(1, 512, 768)
        o_cast(1, 512, 512, 768, True)
        bias(1, 768, 1024, range(4))
        store(1, 768, 1024)
        o_quant(0, 512, 1024)
        store_scales(0, 0, 1024)
        o_quant(1, 0, 512)
        o_cast(1, 768, 768, 1024, False)
        o_quant(1, 512, 1024)
        store_scales(1, 0, 1024)
